import numpy as np
import ml_dtypes


def mxq(x, axis, fmt="e4m3"):
    dtype, down = {"e4m3": (ml_dtypes.float8_e4m3fn, 7), "e5m2": (ml_dtypes.float8_e5m2, 14)}[fmt]
    v = np.moveaxis(np.asarray(x, np.float32).astype(ml_dtypes.bfloat16).astype(np.float64), axis, -1)
    blocks = v.reshape(v.shape[:-1] + (-1, 32))
    amax = np.abs(blocks).max(-1, keepdims=True)
    byte = np.maximum(np.where(amax > 0, np.frexp(amax)[1] - 1 + 127, 0) - down, 1)
    scale = np.exp2(byte - 127.0)
    codes = (blocks / scale).astype(np.float32).astype(dtype).astype(np.float64)
    return np.moveaxis((codes * scale).reshape(v.shape), -1, axis)


WIDE = False


def mx_kscale(k):
    if not WIDE:
        return np.ones(k)
    levels = np.array([10, -10, 5, -5, 0])
    if k % 512:
        return np.exp2(np.random.permutation(np.resize(levels, k // 32))).repeat(32)
    a = np.empty((k // 512, 16))
    for p in range(k // 512):
        a[p, :8] = np.random.permutation(np.resize(levels, 8))
        for g in range(8):
            far = levels[np.abs(levels - a[p, g]) >= 10]
            a[p, g + 8] = far[np.random.randint(len(far))]
    return np.exp2(a.ravel()).repeat(32)


def f64(x):
    return np.asarray(x).astype(np.float64)


def striped(idx):
    return np.tile(idx.reshape(-1, 16).T, (8, 1)).astype(np.uint16)


def unstriped(offs):
    return offs[:16].T.reshape(-1).astype(np.int64)


K, T, S, V, N = 1024, 2048, 512, 256, 256
P = 2 ** 7


def setup_inputs():
    n = np.random.standard_normal
    s = mx_kscale(K)[:, None]
    return {
        "xT": (n((K, T)) * s).astype(np.float32),
        "w1": (n((K, N)) / np.sqrt(K) / s).astype(np.float32),
        "frac": np.tile(np.random.uniform(0.05, 0.95, V), (P, 1)).astype(np.float32),
        "offs": striped(np.random.permutation(T)[:S]),
        "left": striped(np.random.permutation(S)[:V]),
        "right": striped(np.random.permutation(S)[:V]),
    }


def reference(xT, w1, frac, offs, left, right):
    xq = mxq(f64(xT)[:, unstriped(offs)], 0, "e4m3")
    y = mxq(f64(w1), 0, "e4m3").T @ xq
    l = y[:, unstriped(left)]
    return l + (y[:, unstriped(right)] - l) * f64(frac)[:1]

@@ -1,0 +1,149 @@
+from contextlib import ExitStack
+
+import concourse.mybir as mybir
+from concourse.masks import make_identity
+
+K, T, S, V, N = 1024, 2048, 512, 256, 256
+FLOPS = 2 * K * S * N
+
+F32 = mybir.dt.float32
+BF16 = mybir.dt.bfloat16
+U32 = mybir.dt.uint32
+U16 = mybir.dt.uint16
+U8 = mybir.dt.uint8
+FP8X4 = mybir.dt.float8_e4m3fn_x4
+COPY = mybir.ActivationFunctionType.Copy
+MULT = mybir.AluOpType.mult
+ADD = mybir.AluOpType.add
+
+P = 128
+PACK = 4
+K_PASS = P * PACK
+PASSES = K // K_PASS
+BLOCKS = N // P
+HALF = S // 2
+LIST_ROWS = 16
+
+
+def tile_picked_lerp_none_e_kernel(tc, xT, w1, frac, offs, left, right, out):
+    nc = tc.nc
+    with ExitStack() as ctx:
+        keep = ctx.enter_context(tc.tile_pool(name="keep", bufs=1))
+        psum = ctx.enter_context(tc.psum_pool(name="psum", bufs=1))
+
+        x_rows = xT.rearrange("(g p j) t -> g j p t", p=P, j=PACK)
+        w_rows = w1.rearrange("(g p j) m -> g p j m", p=P, j=PACK)
+
+        planes = {}
+
+        def load_plane(g, j):
+            planes[g, j] = keep.tile([P, T], F32, name=f"plane{g}{j}")
+            nc.sync.dma_start(planes[g, j][:], x_rows[g, j])
+
+        load_plane(0, 0)
+        offs_sb = keep.tile([P, S // LIST_ROWS], U16, name="offs_sb")
+        nc.sync.dma_start(offs_sb[:], offs)
+        frac_col = keep.tile([P, 2], F32, name="frac_col")
+        nc.sync.dma_start(frac_col[:], frac[0].rearrange("(p e) -> p e", e=2))
+        for g in range(PASSES):
+            for j in range(PACK):
+                if (g, j) != (0, 0):
+                    load_plane(g, j)
+        w_raw = {}
+        for b in range(BLOCKS):
+            for g in range(PASSES):
+                w_raw[b, g] = keep.tile([P, PACK, P], F32, name=f"w_raw{b}{g}")
+                nc.sync.dma_start(w_raw[b, g][:], w_rows[g, :, :, b * P : (b + 1) * P])
+            if b == 0:
+                left_sb = keep.tile([P, V // LIST_ROWS], U16, name="left_sb")
+                nc.sync.dma_start(left_sb[:], left)
+                right_sb = keep.tile([P, V // LIST_ROWS], U16, name="right_sb")
+                nc.sync.dma_start(right_sb[:], right)
+
+        ident = keep.tile([P, P], F32, name="ident")
+        make_identity(nc, ident[:])
+        frac_ps = psum.tile([P, 2, P], F32, name="frac_ps")
+        for e in range(2):
+            nc.tensor.transpose(frac_ps[:, e, :], frac_col[:, e : e + 1].to_broadcast([P, P]), ident[:])
+        to_right = keep.tile([P, V], F32, name="to_right")
+        to_left = keep.tile([P, V], F32, name="to_left")
+        frac_view = frac_ps[:].rearrange("p e n -> p n e")
+        nc.scalar.activation(to_right[:].rearrange("p (n e) -> p n e", e=2), frac_view, COPY)
+        nc.scalar.activation(to_left[:].rearrange("p (n e) -> p n e", e=2), frac_view, COPY, scale=-1.0, bias=1.0)
+
+        x_codes = [keep.tile([P, S], U32, name=f"x_codes{g}", align_bytes=64) for g in range(PASSES)]
+        x_scales = [keep.tile([P, S], U8, name=f"x_scales{g}", align_bytes=64) for g in range(PASSES)]
+        w_codes, w_scales = {}, {}
+
+        def quantize(codes, scales, grouped):
+            nc.vector.quantize_mx(out=codes.bitcast(FP8X4), scales=scales, in_=grouped.rearrange("p n j -> p (n j)"))
+
+        w_grouped = {}
+
+        def group_w(b, g):
+            w_grouped[b, g] = keep.tile([P, P, PACK], BF16, name=f"w_grouped{b}{g}", align_bytes=64)
+            nc.scalar.copy(
+                w_grouped[b, g][:].rearrange("p (c i) j -> p c j i", i=4),
+                w_raw[b, g][:].rearrange("p j (c i) -> p c j i", i=4),
+            )
+
+        def quantize_w(b, g):
+            w_codes[b, g] = keep.tile([P, P], U32, name=f"w_codes{b}{g}", align_bytes=64)
+            w_scales[b, g] = keep.tile([P, P], U8, name=f"w_scales{b}{g}", align_bytes=64)
+            quantize(w_codes[b, g][:], w_scales[b, g][:], w_grouped[b, g][:])
+
+        def multiply(acc, b, g, cols):
+            nc.tensor.matmul_mx(
+                out=acc,
+                lhsT=w_codes[b, g][:].bitcast(FP8X4),
+                lhsT_scale=w_scales[b, g][:],
+                rhs=x_codes[g][:, cols].bitcast(FP8X4),
+                rhs_scale=x_scales[g][:, cols],
+                start=(g == 0),
+                stop=(g == PASSES - 1),
+            )
+
+        first = keep.tile([P, S, PACK], BF16, name="x_grouped0", align_bytes=64)
+        for j in range(PACK):
+            nc.vector.tensor_copy(first[:, :, j], planes[0, j][:].indirect(offs_sb[:]))
+        quantize(x_codes[0][:], x_scales[0][:], first[:])
+
+        halves = [slice(h * HALF, (h + 1) * HALF) for h in range(2)]
+        last = [keep.tile([P, HALF, PACK], BF16, name=f"x_grouped1{h}", align_bytes=64) for h in range(2)]
+        for j in range(PACK):
+            for h in range(2):
+                part = offs_sb[:, h * HALF // LIST_ROWS : (h + 1) * HALF // LIST_ROWS]
+                nc.vector.tensor_copy(last[h][:, :, j], planes[1, j][:].indirect(part))
+
+        y = [keep.tile([P, S], F32, name=f"y{b}") for b in range(BLOCKS)]
+        acc0 = [psum.tile([P, HALF], F32, name=f"acc0{h}") for h in range(2)]
+        acc1 = psum.tile([P, S], F32, name="acc1")
+
+        group_w(0, 0)
+        group_w(0, 1)
+        group_w(1, 0)
+        quantize_w(0, 0)
+        for h in range(2):
+            multiply(acc0[h][:], 0, 0, halves[h])
+        for h in range(2):
+            quantize(x_codes[1][:, halves[h]], x_scales[1][:, halves[h]], last[h][:])
+        quantize_w(0, 1)
+        for h in range(2):
+            multiply(acc0[h][:], 0, 1, halves[h])
+        quantize_w(1, 0)
+        multiply(acc1[:], 1, 0, slice(0, S))
+        nc.scalar.copy(y[0][:, halves[0]], acc0[0][:])
+        nc.vector.tensor_copy(y[0][:, halves[1]], acc0[1][:])
+        group_w(1, 1)
+        quantize_w(1, 1)
+        multiply(acc1[:], 1, 1, slice(0, S))
+        nc.scalar.copy(y[1][:], acc1[:])
+
+        for b in range(BLOCKS):
+            from_left = keep.tile([P, V], F32, name=f"from_left{b}")
+            from_right = keep.tile([P, V], F32, name=f"from_right{b}")
+            mixed = keep.tile([P, V], F32, name=f"mixed{b}")
+            nc.vector.tensor_tensor(from_left[:], y[b][:].indirect(left_sb[:]), to_left[:], MULT)
+            nc.vector.tensor_tensor(from_right[:], y[b][:].indirect(right_sb[:]), to_right[:], MULT)
+            nc.vector.tensor_tensor(mixed[:], from_left[:], from_right[:], ADD)
+            nc.sync.dma_start(out[b * P : (b + 1) * P, :], mixed[:])

@@ -52,13 +52,12 @@ def tile_picked_lerp_none_e_kernel(tc, xT, w1, frac, offs, left, right, out):
         w_raw = {}
         for b in range(BLOCKS):
             for g in range(PASSES):
-                w_raw[b, g] = keep.tile([P, PACK, P], F32, name=f"w_raw{b}{g}")
+                w_raw[b, g] = keep.tile([P, PACK, P], F32, name=f"w_raw{b}{g}", tag=f"w_raw{b}{g}", align_bytes=64)
                 nc.sync.dma_start(w_raw[b, g][:], w_rows[g, :, :, b * P : (b + 1) * P])
-            if b == 0:
-                left_sb = keep.tile([P, V // LIST_ROWS], U16, name="left_sb")
-                nc.sync.dma_start(left_sb[:], left)
-                right_sb = keep.tile([P, V // LIST_ROWS], U16, name="right_sb")
-                nc.sync.dma_start(right_sb[:], right)
+        left_sb = keep.tile([P, V // LIST_ROWS], U16, name="left_sb")
+        nc.sync.dma_start(left_sb[:], left)
+        right_sb = keep.tile([P, V // LIST_ROWS], U16, name="right_sb")
+        nc.sync.dma_start(right_sb[:], right)
 
         ident = keep.tile([P, P], F32, name="ident")
         make_identity(nc, ident[:])
@@ -66,19 +65,15 @@ def tile_picked_lerp_none_e_kernel(tc, xT, w1, frac, offs, left, right, out):
         for e in range(2):
             nc.tensor.transpose(frac_ps[:, e, :], frac_col[:, e : e + 1].to_broadcast([P, P]), ident[:])
         to_right = keep.tile([P, V], F32, name="to_right")
-        to_left = keep.tile([P, V], F32, name="to_left")
+        to_left = keep.tile([P, V], F32, name="to_left", tag="to_left")
         frac_view = frac_ps[:].rearrange("p e n -> p n e")
         nc.scalar.activation(to_right[:].rearrange("p (n e) -> p n e", e=2), frac_view, COPY)
         nc.scalar.activation(to_left[:].rearrange("p (n e) -> p n e", e=2), frac_view, COPY, scale=-1.0, bias=1.0)
 
-        x_codes = [keep.tile([P, S], U32, name=f"x_codes{g}", align_bytes=64) for g in range(PASSES)]
-        x_scales = [keep.tile([P, S], U8, name=f"x_scales{g}", align_bytes=64) for g in range(PASSES)]
-        w_codes, w_scales = {}, {}
-
         def quantize(codes, scales, grouped):
             nc.vector.quantize_mx(out=codes.bitcast(FP8X4), scales=scales, in_=grouped.rearrange("p n j -> p (n j)"))
 
-        w_grouped = {}
+        w_grouped, w_codes, w_scales = {}, {}, {}
 
         def group_w(b, g):
             w_grouped[b, g] = keep.tile([P, P, PACK], BF16, name=f"w_grouped{b}{g}", align_bytes=64)
@@ -92,13 +87,17 @@ def tile_picked_lerp_none_e_kernel(tc, xT, w1, frac, offs, left, right, out):
             w_scales[b, g] = keep.tile([P, P], U8, name=f"w_scales{b}{g}", align_bytes=64)
             quantize(w_codes[b, g][:], w_scales[b, g][:], w_grouped[b, g][:])
 
-        def multiply(acc, b, g, cols):
+        halves = [slice(h * HALF, (h + 1) * HALF) for h in range(2)]
+        x_codes, x_scales = {}, {}
+        acc = {(b, h): psum.tile([P, HALF], F32, name=f"acc{b}{h}") for b in range(BLOCKS) for h in range(2)}
+
+        def multiply(b, g, h):
             nc.tensor.matmul_mx(
-                out=acc,
+                out=acc[b, h][:],
                 lhsT=w_codes[b, g][:].bitcast(FP8X4),
                 lhsT_scale=w_scales[b, g][:],
-                rhs=x_codes[g][:, cols].bitcast(FP8X4),
-                rhs_scale=x_scales[g][:, cols],
+                rhs=x_codes[g, h].bitcast(FP8X4),
+                rhs_scale=x_scales[g, h],
                 start=(g == 0),
                 stop=(g == PASSES - 1),
             )
@@ -106,44 +105,57 @@ def tile_picked_lerp_none_e_kernel(tc, xT, w1, frac, offs, left, right, out):
         first = keep.tile([P, S, PACK], BF16, name="x_grouped0", align_bytes=64)
         for j in range(PACK):
             nc.vector.tensor_copy(first[:, :, j], planes[0, j][:].indirect(offs_sb[:]))
-        quantize(x_codes[0][:], x_scales[0][:], first[:])
+        first_codes = keep.tile([P, S], U32, name="x_codes0", align_bytes=64)
+        first_scales = keep.tile([P, S], U8, name="x_scales0", align_bytes=64)
+        quantize(first_codes[:], first_scales[:], first[:])
+        for h in range(2):
+            x_codes[0, h], x_scales[0, h] = first_codes[:, halves[h]], first_scales[:, halves[h]]
 
-        halves = [slice(h * HALF, (h + 1) * HALF) for h in range(2)]
         last = [keep.tile([P, HALF, PACK], BF16, name=f"x_grouped1{h}", align_bytes=64) for h in range(2)]
         for j in range(PACK):
             for h in range(2):
                 part = offs_sb[:, h * HALF // LIST_ROWS : (h + 1) * HALF // LIST_ROWS]
                 nc.vector.tensor_copy(last[h][:, :, j], planes[1, j][:].indirect(part))
 
-        y = [keep.tile([P, S], F32, name=f"y{b}") for b in range(BLOCKS)]
-        acc0 = [psum.tile([P, HALF], F32, name=f"acc0{h}") for h in range(2)]
-        acc1 = psum.tile([P, S], F32, name="acc1")
-
-        group_w(0, 0)
-        group_w(0, 1)
-        group_w(1, 0)
-        quantize_w(0, 0)
-        for h in range(2):
-            multiply(acc0[h][:], 0, 0, halves[h])
-        for h in range(2):
-            quantize(x_codes[1][:, halves[h]], x_scales[1][:, halves[h]], last[h][:])
-        quantize_w(0, 1)
-        for h in range(2):
-            multiply(acc0[h][:], 0, 1, halves[h])
-        quantize_w(1, 0)
-        multiply(acc1[:], 1, 0, slice(0, S))
-        nc.scalar.copy(y[0][:, halves[0]], acc0[0][:])
-        nc.vector.tensor_copy(y[0][:, halves[1]], acc0[1][:])
-        group_w(1, 1)
-        quantize_w(1, 1)
-        multiply(acc1[:], 1, 1, slice(0, S))
-        nc.scalar.copy(y[1][:], acc1[:])
-
         for b in range(BLOCKS):
-            from_left = keep.tile([P, V], F32, name=f"from_left{b}")
-            from_right = keep.tile([P, V], F32, name=f"from_right{b}")
-            mixed = keep.tile([P, V], F32, name=f"mixed{b}")
-            nc.vector.tensor_tensor(from_left[:], y[b][:].indirect(left_sb[:]), to_left[:], MULT)
-            nc.vector.tensor_tensor(from_right[:], y[b][:].indirect(right_sb[:]), to_right[:], MULT)
-            nc.vector.tensor_tensor(mixed[:], from_left[:], from_right[:], ADD)
-            nc.sync.dma_start(out[b * P : (b + 1) * P, :], mixed[:])
+            for g in range(PASSES):
+                group_w(b, g)
+
+        def quantize_last(h):
+            codes = keep.tile([P, HALF], U32, name=f"x_codes1{h}", tag=f"w_raw0{h}", align_bytes=64)
+            scales = keep.tile([P, HALF], U8, name=f"x_scales1{h}", align_bytes=64)
+            quantize(codes[:], scales[:], last[h][:])
+            x_codes[1, h], x_scales[1, h] = codes[:], scales[:]
+
+        quantize_w(0, 0)
+        multiply(0, 0, 0)
+        multiply(0, 0, 1)
+        quantize_last(0)
+        quantize_w(0, 1)
+        multiply(0, 1, 0)
+        quantize_last(1)
+        multiply(0, 1, 1)
+        for g in range(PASSES):
+            quantize_w(1, g)
+            multiply(1, g, 0)
+            multiply(1, g, 1)
+
+        y = [
+            keep.tile([P, S], F32, name="y0", tag="w_raw11", align_bytes=64),
+            keep.tile([P, S], F32, name="y1"),
+        ]
+        nc.vector.tensor_copy(y[0][:, halves[0]], acc[0, 0][:])
+        nc.scalar.copy(y[0][:, halves[1]], acc[0, 1][:])
+        for h in range(2):
+            nc.scalar.copy(y[1][:, halves[h]], acc[1, h][:])
+
+        from_left, from_right = [], []
+        for b in range(BLOCKS):
+            from_left.append(keep.tile([P, V], F32, name=f"from_left{b}"))
+            from_right.append(keep.tile([P, V], F32, name=f"from_right{b}"))
+            nc.vector.tensor_tensor(from_left[b][:], y[b][:].indirect(left_sb[:]), to_left[:], MULT)
+            nc.vector.tensor_tensor(from_right[b][:], y[b][:].indirect(right_sb[:]), to_right[:], MULT)
+        mixed = [keep.tile([P, V], F32, name="mixed0", tag="to_left"), keep.tile([P, V], F32, name="mixed1")]
+        for b in range(BLOCKS):
+            nc.vector.tensor_tensor(mixed[b][:], from_left[b][:], from_right[b][:], ADD)
+            nc.sync.dma_start(out[b * P : (b + 1) * P, :], mixed[b][:])

@@ -75,11 +75,11 @@ def tile_picked_lerp_none_e_kernel(tc, xT, w1, frac, offs, left, right, out):
 
         w_grouped, w_codes, w_scales = {}, {}, {}
 
-        def group_w(b, g):
+        def group_w(b, g, copy):
             w_grouped[b, g] = keep.tile([P, P, PACK], BF16, name=f"w_grouped{b}{g}", align_bytes=64)
-            nc.scalar.copy(
-                w_grouped[b, g][:].rearrange("p (c i) j -> p c j i", i=4),
-                w_raw[b, g][:].rearrange("p j (c i) -> p c j i", i=4),
+            copy(
+                w_grouped[b, g][:].rearrange("p (c i) j -> p c j i", i=2),
+                w_raw[b, g][:].rearrange("p j (c i) -> p c j i", i=2),
             )
 
         def quantize_w(b, g):
@@ -117,9 +117,8 @@ def tile_picked_lerp_none_e_kernel(tc, xT, w1, frac, offs, left, right, out):
                 part = offs_sb[:, h * HALF // LIST_ROWS : (h + 1) * HALF // LIST_ROWS]
                 nc.vector.tensor_copy(last[h][:, :, j], planes[1, j][:].indirect(part))
 
-        for b in range(BLOCKS):
-            for g in range(PASSES):
-                group_w(b, g)
+        for b, g in ((0, 0), (0, 1), (1, 0)):
+            group_w(b, g, nc.scalar.copy)
 
         def quantize_last(h):
             codes = keep.tile([P, HALF], U32, name=f"x_codes1{h}", tag=f"w_raw0{h}", align_bytes=64)
@@ -135,16 +134,17 @@ def tile_picked_lerp_none_e_kernel(tc, xT, w1, frac, offs, left, right, out):
         multiply(0, 1, 0)
         quantize_last(1)
         multiply(0, 1, 1)
+        group_w(1, 1, nc.vector.tensor_copy)
         for g in range(PASSES):
             quantize_w(1, g)
             multiply(1, g, 0)
             multiply(1, g, 1)
 
         y = [
-            keep.tile([P, S], F32, name="y0", tag="w_raw11", align_bytes=64),
+            keep.tile([P, S], F32, name="y0"),
             keep.tile([P, S], F32, name="y1"),
         ]
-        nc.vector.tensor_copy(y[0][:, halves[0]], acc[0, 0][:])
+        nc.scalar.copy(y[0][:, halves[0]], acc[0, 0][:])
         nc.scalar.copy(y[0][:, halves[1]], acc[0, 1][:])
         for h in range(2):
             nc.scalar.copy(y[1][:, halves[h]], acc[1, h][:])

@@ -18,11 +18,17 @@ ADD = mybir.AluOpType.add
 
 P = 128
 PACK = 4
-K_PASS = P * PACK
-PASSES = K // K_PASS
+PAIR = 2
+PASSES = K // (P * PACK)
 BLOCKS = N // P
 HALF = S // 2
-LIST_ROWS = 16
+PER_COLUMN = 16
+LINE = 2
+MX_ALIGN = 64
+
+
+def weave(copy, grouped, rows):
+    copy(grouped.rearrange("p (c i) j -> p c j i", i=LINE), rows.rearrange("p j (c i) -> p c j i", i=LINE))
 
 
 def tile_picked_lerp_none_e_kernel(tc, xT, w1, frac, offs, left, right, out):
@@ -31,64 +37,90 @@ def tile_picked_lerp_none_e_kernel(tc, xT, w1, frac, offs, left, right, out):
         keep = ctx.enter_context(tc.tile_pool(name="keep", bufs=1))
         psum = ctx.enter_context(tc.psum_pool(name="psum", bufs=1))
 
-        x_rows = xT.rearrange("(g p j) t -> g j p t", p=P, j=PACK)
+        x_rows = xT.rearrange("(g p j) t -> g p j t", p=P, j=PACK)
         w_rows = w1.rearrange("(g p j) m -> g p j m", p=P, j=PACK)
-
         planes = {}
 
-        def load_plane(g, j):
-            planes[g, j] = keep.tile([P, T], F32, name=f"plane{g}{j}")
-            nc.sync.dma_start(planes[g, j][:], x_rows[g, j])
+        def load_planes(g, j0, count):
+            tile = keep.tile([P, count, T], F32, name=f"planes{g}{j0}")
+            nc.sync.dma_start(tile[:], x_rows[g, :, j0 : j0 + count, :])
+            for j in range(count):
+                planes[g, j0 + j] = tile[:, j, :]
 
-        load_plane(0, 0)
-        offs_sb = keep.tile([P, S // LIST_ROWS], U16, name="offs_sb")
+        load_planes(0, 0, PAIR)
+        offs_sb = keep.tile([P, S // PER_COLUMN], U16, name="offs_sb")
         nc.sync.dma_start(offs_sb[:], offs)
-        frac_col = keep.tile([P, 2], F32, name="frac_col")
-        nc.sync.dma_start(frac_col[:], frac[0].rearrange("(p e) -> p e", e=2))
-        for g in range(PASSES):
-            for j in range(PACK):
-                if (g, j) != (0, 0):
-                    load_plane(g, j)
+        frac_col = keep.tile([P, V // P], F32, name="frac_col")
+        nc.sync.dma_start(frac_col[:], frac[0].rearrange("(n e) -> n e", n=P))
+        load_planes(0, PAIR, PAIR)
+        for j in range(PACK):
+            load_planes(1, j, 1)
         w_raw = {}
         for b in range(BLOCKS):
             for g in range(PASSES):
-                w_raw[b, g] = keep.tile([P, PACK, P], F32, name=f"w_raw{b}{g}", tag=f"w_raw{b}{g}", align_bytes=64)
+                w_raw[b, g] = keep.tile([P, PACK, P], F32, name=f"w_raw{b}{g}", align_bytes=MX_ALIGN)
                 nc.sync.dma_start(w_raw[b, g][:], w_rows[g, :, :, b * P : (b + 1) * P])
-        left_sb = keep.tile([P, V // LIST_ROWS], U16, name="left_sb")
+        left_sb = keep.tile([P, V // PER_COLUMN], U16, name="left_sb")
         nc.sync.dma_start(left_sb[:], left)
-        right_sb = keep.tile([P, V // LIST_ROWS], U16, name="right_sb")
+        right_sb = keep.tile([P, V // PER_COLUMN], U16, name="right_sb")
         nc.sync.dma_start(right_sb[:], right)
 
         ident = keep.tile([P, P], F32, name="ident")
         make_identity(nc, ident[:])
-        frac_ps = psum.tile([P, 2, P], F32, name="frac_ps")
-        for e in range(2):
+        frac_ps = psum.tile([P, V // P, P], F32, name="frac_ps")
+        for e in range(V // P):
             nc.tensor.transpose(frac_ps[:, e, :], frac_col[:, e : e + 1].to_broadcast([P, P]), ident[:])
         to_right = keep.tile([P, V], F32, name="to_right")
-        to_left = keep.tile([P, V], F32, name="to_left", tag="to_left")
+        to_left = keep.tile([P, V], F32, name="to_left")
         frac_view = frac_ps[:].rearrange("p e n -> p n e")
-        nc.scalar.activation(to_right[:].rearrange("p (n e) -> p n e", e=2), frac_view, COPY)
-        nc.scalar.activation(to_left[:].rearrange("p (n e) -> p n e", e=2), frac_view, COPY, scale=-1.0, bias=1.0)
+        nc.scalar.activation(to_right[:].rearrange("p (n e) -> p n e", n=P), frac_view, COPY)
+        nc.scalar.activation(to_left[:].rearrange("p (n e) -> p n e", n=P), frac_view, COPY, scale=-1.0, bias=1.0)
 
         def quantize(codes, scales, grouped):
             nc.vector.quantize_mx(out=codes.bitcast(FP8X4), scales=scales, in_=grouped.rearrange("p n j -> p (n j)"))
 
+        halves = [slice(0, HALF), slice(HALF, S)]
+        x_codes, x_scales = {}, {}
+
+        grouped0 = keep.tile([P, S, PACK], BF16, name="grouped0", align_bytes=MX_ALIGN)
+        picked0 = keep.tile([P, PACK, S], F32, name="picked0")
+        for j in range(PACK):
+            nc.vector.tensor_copy(picked0[:, j, :], planes[0, j].indirect(offs_sb[:]))
+        weave(nc.scalar.copy, grouped0[:], picked0[:])
+        codes0 = keep.tile([P, S], U32, name="codes0", align_bytes=MX_ALIGN)
+        scales0 = keep.tile([P, S], U8, name="scales0", align_bytes=MX_ALIGN)
+        quantize(codes0[:], scales0[:], grouped0[:])
+        for h, cols in enumerate(halves):
+            x_codes[0, h], x_scales[0, h] = codes0[:, cols], scales0[:, cols]
+
+        grouped1 = [keep.tile([P, HALF, PACK], BF16, name=f"grouped1{h}", align_bytes=MX_ALIGN) for h in range(2)]
+        picked1 = keep.tile([P, PAIR, S], F32, name="picked1")
+        for j in range(PAIR):
+            nc.vector.tensor_copy(picked1[:, j, :], planes[1, j].indirect(offs_sb[:]))
+        for h, cols in enumerate(halves):
+            weave(nc.scalar.copy, grouped1[h][:, :, 0:PAIR], picked1[:, :, cols])
+        for j in range(PAIR, PACK):
+            for h, cols in enumerate(halves):
+                entries = offs_sb[:, cols.start // PER_COLUMN : cols.stop // PER_COLUMN]
+                nc.vector.tensor_copy(grouped1[h][:, :, j], planes[1, j].indirect(entries))
+
         w_grouped, w_codes, w_scales = {}, {}, {}
 
         def group_w(b, g, copy):
-            w_grouped[b, g] = keep.tile([P, P, PACK], BF16, name=f"w_grouped{b}{g}", align_bytes=64)
-            copy(
-                w_grouped[b, g][:].rearrange("p (c i) j -> p c j i", i=2),
-                w_raw[b, g][:].rearrange("p j (c i) -> p c j i", i=2),
-            )
+            w_grouped[b, g] = keep.tile([P, P, PACK], BF16, name=f"w_grouped{b}{g}", align_bytes=MX_ALIGN)
+            weave(copy, w_grouped[b, g][:], w_raw[b, g][:])
 
         def quantize_w(b, g):
-            w_codes[b, g] = keep.tile([P, P], U32, name=f"w_codes{b}{g}", align_bytes=64)
-            w_scales[b, g] = keep.tile([P, P], U8, name=f"w_scales{b}{g}", align_bytes=64)
+            w_codes[b, g] = keep.tile([P, P], U32, name=f"w_codes{b}{g}", align_bytes=MX_ALIGN)
+            w_scales[b, g] = keep.tile([P, P], U8, name=f"w_scales{b}{g}", align_bytes=MX_ALIGN)
             quantize(w_codes[b, g][:], w_scales[b, g][:], w_grouped[b, g][:])
 
-        halves = [slice(h * HALF, (h + 1) * HALF) for h in range(2)]
-        x_codes, x_scales = {}, {}
+        def quantize_half(h):
+            codes = keep.tile([P, HALF], U32, name=f"codes1{h}", tag=f"w_raw0{h}", align_bytes=MX_ALIGN)
+            scales = keep.tile([P, HALF], U8, name=f"scales1{h}", align_bytes=MX_ALIGN)
+            quantize(codes[:], scales[:], grouped1[h][:])
+            x_codes[1, h], x_scales[1, h] = codes[:], scales[:]
+
         acc = {(b, h): psum.tile([P, HALF], F32, name=f"acc{b}{h}") for b in range(BLOCKS) for h in range(2)}
 
         def multiply(b, g, h):
@@ -102,37 +134,16 @@ def tile_picked_lerp_none_e_kernel(tc, xT, w1, frac, offs, left, right, out):
                 stop=(g == PASSES - 1),
             )
 
-        first = keep.tile([P, S, PACK], BF16, name="x_grouped0", align_bytes=64)
-        for j in range(PACK):
-            nc.vector.tensor_copy(first[:, :, j], planes[0, j][:].indirect(offs_sb[:]))
-        first_codes = keep.tile([P, S], U32, name="x_codes0", align_bytes=64)
-        first_scales = keep.tile([P, S], U8, name="x_scales0", align_bytes=64)
-        quantize(first_codes[:], first_scales[:], first[:])
-        for h in range(2):
-            x_codes[0, h], x_scales[0, h] = first_codes[:, halves[h]], first_scales[:, halves[h]]
-
-        last = [keep.tile([P, HALF, PACK], BF16, name=f"x_grouped1{h}", align_bytes=64) for h in range(2)]
-        for j in range(PACK):
-            for h in range(2):
-                part = offs_sb[:, h * HALF // LIST_ROWS : (h + 1) * HALF // LIST_ROWS]
-                nc.vector.tensor_copy(last[h][:, :, j], planes[1, j][:].indirect(part))
-
-        for b, g in ((0, 0), (0, 1), (1, 0)):
-            group_w(b, g, nc.scalar.copy)
-
-        def quantize_last(h):
-            codes = keep.tile([P, HALF], U32, name=f"x_codes1{h}", tag=f"w_raw0{h}", align_bytes=64)
-            scales = keep.tile([P, HALF], U8, name=f"x_scales1{h}", align_bytes=64)
-            quantize(codes[:], scales[:], last[h][:])
-            x_codes[1, h], x_scales[1, h] = codes[:], scales[:]
-
+        group_w(0, 0, nc.scalar.copy)
+        group_w(0, 1, nc.scalar.copy)
+        group_w(1, 0, nc.scalar.copy)
         quantize_w(0, 0)
         multiply(0, 0, 0)
         multiply(0, 0, 1)
-        quantize_last(0)
+        quantize_half(0)
         quantize_w(0, 1)
         multiply(0, 1, 0)
-        quantize_last(1)
+        quantize_half(1)
         multiply(0, 1, 1)
         group_w(1, 1, nc.vector.tensor_copy)
         for g in range(PASSES):
@@ -140,14 +151,10 @@ def tile_picked_lerp_none_e_kernel(tc, xT, w1, frac, offs, left, right, out):
             multiply(1, g, 0)
             multiply(1, g, 1)
 
-        y = [
-            keep.tile([P, S], F32, name="y0"),
-            keep.tile([P, S], F32, name="y1"),
-        ]
-        nc.scalar.copy(y[0][:, halves[0]], acc[0, 0][:])
-        nc.scalar.copy(y[0][:, halves[1]], acc[0, 1][:])
-        for h in range(2):
-            nc.scalar.copy(y[1][:, halves[h]], acc[1, h][:])
+        y = [keep.tile([P, S], F32, name=f"y{b}") for b in range(BLOCKS)]
+        for b in range(BLOCKS):
+            for h, cols in enumerate(halves):
+                nc.scalar.copy(y[b][:, cols], acc[b, h][:])
 
         from_left, from_right = [], []
         for b in range(BLOCKS):

@@ -25,6 +25,7 @@ HALF = S // 2
 PER_COLUMN = 16
 LINE = 2
 MX_ALIGN = 64
+DMA_ALIGN = 256
 
 
 def weave(copy, grouped, rows):
@@ -42,7 +43,7 @@ def tile_picked_lerp_none_e_kernel(tc, xT, w1, frac, offs, left, right, out):
         planes = {}
 
         def load_planes(g, j0, count):
-            tile = keep.tile([P, count, T], F32, name=f"planes{g}{j0}")
+            tile = keep.tile([P, count, T], F32, name=f"planes{g}{j0}", align_bytes=DMA_ALIGN)
             nc.sync.dma_start(tile[:], x_rows[g, :, j0 : j0 + count, :])
             for j in range(count):
                 planes[g, j0 + j] = tile[:, j, :]
@@ -58,7 +59,7 @@ def tile_picked_lerp_none_e_kernel(tc, xT, w1, frac, offs, left, right, out):
         w_raw = {}
         for b in range(BLOCKS):
             for g in range(PASSES):
-                w_raw[b, g] = keep.tile([P, PACK, P], F32, name=f"w_raw{b}{g}", align_bytes=MX_ALIGN)
+                w_raw[b, g] = keep.tile([P, PACK, P], F32, name=f"w_raw{b}{g}", align_bytes=DMA_ALIGN)
                 nc.sync.dma_start(w_raw[b, g][:], w_rows[g, :, :, b * P : (b + 1) * P])
         left_sb = keep.tile([P, V // PER_COLUMN], U16, name="left_sb")
         nc.sync.dma_start(left_sb[:], left)
@@ -71,7 +72,7 @@ def tile_picked_lerp_none_e_kernel(tc, xT, w1, frac, offs, left, right, out):
         for e in range(V // P):
             nc.tensor.transpose(frac_ps[:, e, :], frac_col[:, e : e + 1].to_broadcast([P, P]), ident[:])
         to_right = keep.tile([P, V], F32, name="to_right")
-        to_left = keep.tile([P, V], F32, name="to_left")
+        to_left = keep.tile([P, V], F32, name="to_left", align_bytes=DMA_ALIGN)
         frac_view = frac_ps[:].rearrange("p e n -> p n e")
         nc.scalar.activation(to_right[:].rearrange("p (n e) -> p n e", n=P), frac_view, COPY)
         nc.scalar.activation(to_left[:].rearrange("p (n e) -> p n e", n=P), frac_view, COPY, scale=-1.0, bias=1.0)
@@ -116,7 +117,7 @@ def tile_picked_lerp_none_e_kernel(tc, xT, w1, frac, offs, left, right, out):
             quantize(w_codes[b, g][:], w_scales[b, g][:], w_grouped[b, g][:])
 
         def quantize_half(h):
-            codes = keep.tile([P, HALF], U32, name=f"codes1{h}", tag=f"w_raw0{h}", align_bytes=MX_ALIGN)
+            codes = keep.tile([P, HALF], U32, name=f"codes1{h}", tag=f"w_raw0{h}", align_bytes=DMA_ALIGN)
             scales = keep.tile([P, HALF], U8, name=f"scales1{h}", align_bytes=MX_ALIGN)
             quantize(codes[:], scales[:], grouped1[h][:])
             x_codes[1, h], x_scales[1, h] = codes[:], scales[:]
@@ -162,7 +163,10 @@ def tile_picked_lerp_none_e_kernel(tc, xT, w1, frac, offs, left, right, out):
             from_right.append(keep.tile([P, V], F32, name=f"from_right{b}"))
             nc.vector.tensor_tensor(from_left[b][:], y[b][:].indirect(left_sb[:]), to_left[:], MULT)
             nc.vector.tensor_tensor(from_right[b][:], y[b][:].indirect(right_sb[:]), to_right[:], MULT)
-        mixed = [keep.tile([P, V], F32, name="mixed0", tag="to_left"), keep.tile([P, V], F32, name="mixed1")]
+        mixed = [
+            keep.tile([P, V], F32, name="mixed0", tag="to_left", align_bytes=DMA_ALIGN),
+            keep.tile([P, V], F32, name="mixed1", align_bytes=DMA_ALIGN),
+        ]
         for b in range(BLOCKS):
             nc.vector.tensor_tensor(mixed[b][:], from_left[b][:], from_right[b][:], ADD)
             nc.sync.dma_start(out[b * P : (b + 1) * P, :], mixed[b][:])

@@ -1,7 +1,6 @@
 from contextlib import ExitStack
 
 import concourse.mybir as mybir
-from concourse.masks import make_identity
 
 K, T, S, V, N = 1024, 2048, 512, 256, 256
 FLOPS = 2 * K * S * N
@@ -12,7 +11,6 @@ U32 = mybir.dt.uint32
 U16 = mybir.dt.uint16
 U8 = mybir.dt.uint8
 FP8X4 = mybir.dt.float8_e4m3fn_x4
-COPY = mybir.ActivationFunctionType.Copy
 MULT = mybir.AluOpType.mult
 ADD = mybir.AluOpType.add
 
@@ -24,8 +22,7 @@ BLOCKS = N // P
 HALF = S // 2
 PER_COLUMN = 16
 LINE = 2
-MX_ALIGN = 64
-DMA_ALIGN = 256
+ALIGN = 256
 
 
 def weave(copy, grouped, rows):
@@ -35,47 +32,39 @@ def weave(copy, grouped, rows):
 def tile_picked_lerp_none_e_kernel(tc, xT, w1, frac, offs, left, right, out):
     nc = tc.nc
     with ExitStack() as ctx:
-        keep = ctx.enter_context(tc.tile_pool(name="keep", bufs=1))
+        pool = ctx.enter_context(tc.tile_pool(name="keep", bufs=1))
         psum = ctx.enter_context(tc.psum_pool(name="psum", bufs=1))
+
+        def keep(shape, dtype, name, tag=""):
+            return pool.tile(shape, dtype, name=name, tag=tag, align_bytes=ALIGN)
 
         x_rows = xT.rearrange("(g p j) t -> g p j t", p=P, j=PACK)
         w_rows = w1.rearrange("(g p j) m -> g p j m", p=P, j=PACK)
         planes = {}
 
         def load_planes(g, j0, count):
-            tile = keep.tile([P, count, T], F32, name=f"planes{g}{j0}", align_bytes=DMA_ALIGN)
+            tile = keep([P, count, T], F32, name=f"planes{g}{j0}")
             nc.sync.dma_start(tile[:], x_rows[g, :, j0 : j0 + count, :])
             for j in range(count):
                 planes[g, j0 + j] = tile[:, j, :]
 
         load_planes(0, 0, PAIR)
-        offs_sb = keep.tile([P, S // PER_COLUMN], U16, name="offs_sb")
+        offs_sb = keep([P, S // PER_COLUMN], U16, name="offs_sb")
         nc.sync.dma_start(offs_sb[:], offs)
-        frac_col = keep.tile([P, V // P], F32, name="frac_col")
-        nc.sync.dma_start(frac_col[:], frac[0].rearrange("(n e) -> n e", n=P))
         load_planes(0, PAIR, PAIR)
         for j in range(PACK):
             load_planes(1, j, 1)
         w_raw = {}
         for b in range(BLOCKS):
             for g in range(PASSES):
-                w_raw[b, g] = keep.tile([P, PACK, P], F32, name=f"w_raw{b}{g}", align_bytes=DMA_ALIGN)
+                w_raw[b, g] = keep([P, PACK, P], F32, name=f"w_raw{b}{g}")
                 nc.sync.dma_start(w_raw[b, g][:], w_rows[g, :, :, b * P : (b + 1) * P])
-        left_sb = keep.tile([P, V // PER_COLUMN], U16, name="left_sb")
+        to_right = keep([P, V], F32, name="to_right")
+        nc.sync.dma_start(to_right[:], frac)
+        left_sb = keep([P, V // PER_COLUMN], U16, name="left_sb")
         nc.sync.dma_start(left_sb[:], left)
-        right_sb = keep.tile([P, V // PER_COLUMN], U16, name="right_sb")
+        right_sb = keep([P, V // PER_COLUMN], U16, name="right_sb")
         nc.sync.dma_start(right_sb[:], right)
-
-        ident = keep.tile([P, P], F32, name="ident")
-        make_identity(nc, ident[:])
-        frac_ps = psum.tile([P, V // P, P], F32, name="frac_ps")
-        for e in range(V // P):
-            nc.tensor.transpose(frac_ps[:, e, :], frac_col[:, e : e + 1].to_broadcast([P, P]), ident[:])
-        to_right = keep.tile([P, V], F32, name="to_right")
-        to_left = keep.tile([P, V], F32, name="to_left", align_bytes=DMA_ALIGN)
-        frac_view = frac_ps[:].rearrange("p e n -> p n e")
-        nc.scalar.activation(to_right[:].rearrange("p (n e) -> p n e", n=P), frac_view, COPY)
-        nc.scalar.activation(to_left[:].rearrange("p (n e) -> p n e", n=P), frac_view, COPY, scale=-1.0, bias=1.0)
 
         def quantize(codes, scales, grouped):
             nc.vector.quantize_mx(out=codes.bitcast(FP8X4), scales=scales, in_=grouped.rearrange("p n j -> p (n j)"))
@@ -83,19 +72,19 @@ def tile_picked_lerp_none_e_kernel(tc, xT, w1, frac, offs, left, right, out):
         halves = [slice(0, HALF), slice(HALF, S)]
         x_codes, x_scales = {}, {}
 
-        grouped0 = keep.tile([P, S, PACK], BF16, name="grouped0", align_bytes=MX_ALIGN)
-        picked0 = keep.tile([P, PACK, S], F32, name="picked0")
+        grouped0 = keep([P, S, PACK], BF16, name="grouped0")
+        picked0 = keep([P, PACK, S], F32, name="picked0")
         for j in range(PACK):
             nc.vector.tensor_copy(picked0[:, j, :], planes[0, j].indirect(offs_sb[:]))
         weave(nc.scalar.copy, grouped0[:], picked0[:])
-        codes0 = keep.tile([P, S], U32, name="codes0", align_bytes=MX_ALIGN)
-        scales0 = keep.tile([P, S], U8, name="scales0", align_bytes=MX_ALIGN)
+        codes0 = keep([P, S], U32, name="codes0")
+        scales0 = keep([P, S], U8, name="scales0")
         quantize(codes0[:], scales0[:], grouped0[:])
         for h, cols in enumerate(halves):
             x_codes[0, h], x_scales[0, h] = codes0[:, cols], scales0[:, cols]
 
-        grouped1 = [keep.tile([P, HALF, PACK], BF16, name=f"grouped1{h}", align_bytes=MX_ALIGN) for h in range(2)]
-        picked1 = keep.tile([P, PAIR, S], F32, name="picked1")
+        grouped1 = [keep([P, HALF, PACK], BF16, name=f"grouped1{h}") for h in range(2)]
+        picked1 = keep([P, PAIR, S], F32, name="picked1")
         for j in range(PAIR):
             nc.vector.tensor_copy(picked1[:, j, :], planes[1, j].indirect(offs_sb[:]))
         for h, cols in enumerate(halves):
@@ -108,17 +97,17 @@ def tile_picked_lerp_none_e_kernel(tc, xT, w1, frac, offs, left, right, out):
         w_grouped, w_codes, w_scales = {}, {}, {}
 
         def group_w(b, g, copy):
-            w_grouped[b, g] = keep.tile([P, P, PACK], BF16, name=f"w_grouped{b}{g}", align_bytes=MX_ALIGN)
+            w_grouped[b, g] = keep([P, P, PACK], BF16, name=f"w_grouped{b}{g}")
             weave(copy, w_grouped[b, g][:], w_raw[b, g][:])
 
         def quantize_w(b, g):
-            w_codes[b, g] = keep.tile([P, P], U32, name=f"w_codes{b}{g}", align_bytes=MX_ALIGN)
-            w_scales[b, g] = keep.tile([P, P], U8, name=f"w_scales{b}{g}", align_bytes=MX_ALIGN)
+            w_codes[b, g] = keep([P, P], U32, name=f"w_codes{b}{g}")
+            w_scales[b, g] = keep([P, P], U8, name=f"w_scales{b}{g}")
             quantize(w_codes[b, g][:], w_scales[b, g][:], w_grouped[b, g][:])
 
         def quantize_half(h):
-            codes = keep.tile([P, HALF], U32, name=f"codes1{h}", tag=f"w_raw0{h}", align_bytes=DMA_ALIGN)
-            scales = keep.tile([P, HALF], U8, name=f"scales1{h}", align_bytes=MX_ALIGN)
+            codes = keep([P, HALF], U32, name=f"codes1{h}", tag=f"w_raw0{h}")
+            scales = keep([P, HALF], U8, name=f"scales1{h}")
             quantize(codes[:], scales[:], grouped1[h][:])
             x_codes[1, h], x_scales[1, h] = codes[:], scales[:]
 
@@ -152,21 +141,21 @@ def tile_picked_lerp_none_e_kernel(tc, xT, w1, frac, offs, left, right, out):
             multiply(1, g, 0)
             multiply(1, g, 1)
 
-        y = [keep.tile([P, S], F32, name=f"y{b}") for b in range(BLOCKS)]
+        to_left = keep([P, V], F32, name="to_left", tag="w_grouped11")
+        nc.vector.tensor_scalar(to_left[:], to_right[:], -1.0, 1.0, MULT, ADD)
+
+        y = [keep([P, S], F32, name=f"y{b}") for b in range(BLOCKS)]
         for b in range(BLOCKS):
             for h, cols in enumerate(halves):
                 nc.scalar.copy(y[b][:, cols], acc[b, h][:])
 
         from_left, from_right = [], []
         for b in range(BLOCKS):
-            from_left.append(keep.tile([P, V], F32, name=f"from_left{b}"))
-            from_right.append(keep.tile([P, V], F32, name=f"from_right{b}"))
+            from_left.append(keep([P, V], F32, name=f"from_left{b}"))
+            from_right.append(keep([P, V], F32, name=f"from_right{b}"))
             nc.vector.tensor_tensor(from_left[b][:], y[b][:].indirect(left_sb[:]), to_left[:], MULT)
             nc.vector.tensor_tensor(from_right[b][:], y[b][:].indirect(right_sb[:]), to_right[:], MULT)
-        mixed = [
-            keep.tile([P, V], F32, name="mixed0", tag="to_left", align_bytes=DMA_ALIGN),
-            keep.tile([P, V], F32, name="mixed1", align_bytes=DMA_ALIGN),
-        ]
+        mixed = [keep([P, V], F32, name="mixed0", tag="w_grouped11"), keep([P, V], F32, name="mixed1")]
         for b in range(BLOCKS):
             nc.vector.tensor_tensor(mixed[b][:], from_left[b][:], from_right[b][:], ADD)
             nc.sync.dma_start(out[b * P : (b + 1) * P, :], mixed[b][:])

@@ -96,8 +96,8 @@ def tile_picked_lerp_none_e_kernel(tc, xT, w1, frac, offs, left, right, out):
 
         w_grouped, w_codes, w_scales = {}, {}, {}
 
-        def group_w(b, g, copy):
-            w_grouped[b, g] = keep([P, P, PACK], BF16, name=f"w_grouped{b}{g}")
+        def group_w(b, g, copy, tag=""):
+            w_grouped[b, g] = keep([P, P, PACK], BF16, name=f"w_grouped{b}{g}", tag=tag)
             weave(copy, w_grouped[b, g][:], w_raw[b, g][:])
 
         def quantize_w(b, g):
@@ -135,14 +135,15 @@ def tile_picked_lerp_none_e_kernel(tc, xT, w1, frac, offs, left, right, out):
         multiply(0, 1, 0)
         quantize_half(1)
         multiply(0, 1, 1)
-        group_w(1, 1, nc.vector.tensor_copy)
-        for g in range(PASSES):
-            quantize_w(1, g)
-            multiply(1, g, 0)
-            multiply(1, g, 1)
-
-        to_left = keep([P, V], F32, name="to_left", tag="w_grouped11")
+        quantize_w(1, 0)
+        multiply(1, 0, 0)
+        multiply(1, 0, 1)
+        group_w(1, 1, nc.vector.tensor_copy, tag="w_raw10")
+        to_left = keep([P, V], F32, name="to_left", tag="w_grouped10")
         nc.vector.tensor_scalar(to_left[:], to_right[:], -1.0, 1.0, MULT, ADD)
+        quantize_w(1, 1)
+        multiply(1, 1, 0)
+        multiply(1, 1, 1)
 
         y = [keep([P, S], F32, name=f"y{b}") for b in range(BLOCKS)]
         for b in range(BLOCKS):
@@ -155,7 +156,7 @@ def tile_picked_lerp_none_e_kernel(tc, xT, w1, frac, offs, left, right, out):
             from_right.append(keep([P, V], F32, name=f"from_right{b}"))
             nc.vector.tensor_tensor(from_left[b][:], y[b][:].indirect(left_sb[:]), to_left[:], MULT)
             nc.vector.tensor_tensor(from_right[b][:], y[b][:].indirect(right_sb[:]), to_right[:], MULT)
-        mixed = [keep([P, V], F32, name="mixed0", tag="w_grouped11"), keep([P, V], F32, name="mixed1")]
+        mixed = [keep([P, V], F32, name="mixed0", tag="w_grouped10"), keep([P, V], F32, name="mixed1")]
         for b in range(BLOCKS):
             nc.vector.tensor_tensor(mixed[b][:], from_left[b][:], from_right[b][:], ADD)
             nc.sync.dma_start(out[b * P : (b + 1) * P, :], mixed[b][:])

@@ -77,11 +77,6 @@ def tile_picked_lerp_none_e_kernel(tc, xT, w1, frac, offs, left, right, out):
         for j in range(PACK):
             nc.vector.tensor_copy(picked0[:, j, :], planes[0, j].indirect(offs_sb[:]))
         weave(nc.scalar.copy, grouped0[:], picked0[:])
-        codes0 = keep([P, S], U32, name="codes0")
-        scales0 = keep([P, S], U8, name="scales0")
-        quantize(codes0[:], scales0[:], grouped0[:])
-        for h, cols in enumerate(halves):
-            x_codes[0, h], x_scales[0, h] = codes0[:, cols], scales0[:, cols]
 
         grouped1 = [keep([P, HALF, PACK], BF16, name=f"grouped1{h}") for h in range(2)]
         picked1 = keep([P, PAIR, S], F32, name="picked1")
@@ -89,6 +84,11 @@ def tile_picked_lerp_none_e_kernel(tc, xT, w1, frac, offs, left, right, out):
             nc.vector.tensor_copy(picked1[:, j, :], planes[1, j].indirect(offs_sb[:]))
         for h, cols in enumerate(halves):
             weave(nc.scalar.copy, grouped1[h][:, :, 0:PAIR], picked1[:, :, cols])
+        codes0 = keep([P, S], U32, name="codes0", tag="planes11")
+        scales0 = keep([P, S], U8, name="scales0")
+        quantize(codes0[:], scales0[:], grouped0[:])
+        for h, cols in enumerate(halves):
+            x_codes[0, h], x_scales[0, h] = codes0[:, cols], scales0[:, cols]
         for j in range(PAIR, PACK):
             for h, cols in enumerate(halves):
                 entries = offs_sb[:, cols.start // PER_COLUMN : cols.stop // PER_COLUMN]

@@ -20,6 +20,7 @@ PAIR = 2
 PASSES = K // (P * PACK)
 BLOCKS = N // P
 HALF = S // 2
+QUARTER = S // 4
 PER_COLUMN = 16
 LINE = 2
 ALIGN = 256
@@ -70,6 +71,7 @@ def tile_picked_lerp_none_e_kernel(tc, xT, w1, frac, offs, left, right, out):
             nc.vector.quantize_mx(out=codes.bitcast(FP8X4), scales=scales, in_=grouped.rearrange("p n j -> p (n j)"))
 
         halves = [slice(0, HALF), slice(HALF, S)]
+        quarters = [slice(q * QUARTER, (q + 1) * QUARTER) for q in range(4)]
         x_codes, x_scales = {}, {}
 
         grouped0 = keep([P, S, PACK], BF16, name="grouped0")
@@ -87,8 +89,8 @@ def tile_picked_lerp_none_e_kernel(tc, xT, w1, frac, offs, left, right, out):
         codes0 = keep([P, S], U32, name="codes0", tag="planes11")
         scales0 = keep([P, S], U8, name="scales0")
         quantize(codes0[:], scales0[:], grouped0[:])
-        for h, cols in enumerate(halves):
-            x_codes[0, h], x_scales[0, h] = codes0[:, cols], scales0[:, cols]
+        for q, cols in enumerate(quarters):
+            x_codes[0, q], x_scales[0, q] = codes0[:, cols], scales0[:, cols]
         for j in range(PAIR, PACK):
             for h, cols in enumerate(halves):
                 entries = offs_sb[:, cols.start // PER_COLUMN : cols.stop // PER_COLUMN]
@@ -108,21 +110,24 @@ def tile_picked_lerp_none_e_kernel(tc, xT, w1, frac, offs, left, right, out):
         def quantize_half(h):
             codes = keep([P, HALF], U32, name=f"codes1{h}", tag=f"w_raw0{h}")
             scales = keep([P, HALF], U8, name=f"scales1{h}")
-            quantize(codes[:], scales[:], grouped1[h][:])
-            x_codes[1, h], x_scales[1, h] = codes[:], scales[:]
+            for i in range(2):
+                cols = slice(i * QUARTER, (i + 1) * QUARTER)
+                quantize(codes[:, cols], scales[:, cols], grouped1[h][:, cols, :])
+                x_codes[1, 2 * h + i], x_scales[1, 2 * h + i] = codes[:, cols], scales[:, cols]
 
-        acc = {(b, h): psum.tile([P, HALF], F32, name=f"acc{b}{h}") for b in range(BLOCKS) for h in range(2)}
+        acc = {(b, q): psum.tile([P, QUARTER], F32, name=f"acc{b}{q}") for b in range(BLOCKS) for q in range(4)}
 
         def multiply(b, g, h):
-            nc.tensor.matmul_mx(
-                out=acc[b, h][:],
-                lhsT=w_codes[b, g][:].bitcast(FP8X4),
-                lhsT_scale=w_scales[b, g][:],
-                rhs=x_codes[g, h].bitcast(FP8X4),
-                rhs_scale=x_scales[g, h],
-                start=(g == 0),
-                stop=(g == PASSES - 1),
-            )
+            for q in (2 * h, 2 * h + 1):
+                nc.tensor.matmul_mx(
+                    out=acc[b, q][:],
+                    lhsT=w_codes[b, g][:].bitcast(FP8X4),
+                    lhsT_scale=w_scales[b, g][:],
+                    rhs=x_codes[g, q].bitcast(FP8X4),
+                    rhs_scale=x_scales[g, q],
+                    start=(g == 0),
+                    stop=(g == PASSES - 1),
+                )
 
         group_w(0, 0, nc.scalar.copy)
         group_w(0, 1, nc.scalar.copy)
@@ -147,8 +152,8 @@ def tile_picked_lerp_none_e_kernel(tc, xT, w1, frac, offs, left, right, out):
 
         y = [keep([P, S], F32, name=f"y{b}") for b in range(BLOCKS)]
         for b in range(BLOCKS):
-            for h, cols in enumerate(halves):
-                nc.scalar.copy(y[b][:, cols], acc[b, h][:])
+            for q, cols in enumerate(quarters):
+                nc.scalar.copy(y[b][:, cols], acc[b, q][:])
 
         from_left, from_right = [], []
         for b in range(BLOCKS):

@@ -143,10 +143,16 @@ def tile_picked_lerp_none_e_kernel(tc, xT, w1, frac, offs, left, right, out):
         quantize_w(1, 0)
         multiply(1, 0, 0)
         multiply(1, 0, 1)
-        group_w(1, 1, nc.vector.tensor_copy, tag="w_raw10")
+        w_grouped[1, 1] = keep([P, P, PACK], BF16, name="w_grouped11", tag="w_raw10")
+        column_halves = [slice(0, P // 2), slice(P // 2, P)]
+        for cols in column_halves:
+            weave(nc.vector.tensor_copy, w_grouped[1, 1][:, cols, :], w_raw[1, 1][:, :, cols])
         to_left = keep([P, V], F32, name="to_left", tag="w_grouped10")
         nc.vector.tensor_scalar(to_left[:], to_right[:], -1.0, 1.0, MULT, ADD)
-        quantize_w(1, 1)
+        w_codes[1, 1] = keep([P, P], U32, name="w_codes11")
+        w_scales[1, 1] = keep([P, P], U8, name="w_scales11")
+        for cols in column_halves:
+            quantize(w_codes[1, 1][:, cols], w_scales[1, 1][:, cols], w_grouped[1, 1][:, cols, :])
         multiply(1, 1, 0)
         multiply(1, 1, 1)
 

@@ -53,19 +53,22 @@ def tile_picked_lerp_none_e_kernel(tc, xT, w1, frac, offs, left, right, out):
         offs_sb = keep([P, S // PER_COLUMN], U16, name="offs_sb")
         nc.sync.dma_start(offs_sb[:], offs)
         load_planes(0, PAIR, PAIR)
-        for j in range(PACK):
+        load_planes(1, 0, PAIR)
+        for j in range(PAIR, PACK):
             load_planes(1, j, 1)
         w_raw = {}
         for b in range(BLOCKS):
             for g in range(PASSES):
                 w_raw[b, g] = keep([P, PACK, P], F32, name=f"w_raw{b}{g}")
-                nc.sync.dma_start(w_raw[b, g][:], w_rows[g, :, :, b * P : (b + 1) * P])
-        to_right = keep([P, V], F32, name="to_right")
-        nc.sync.dma_start(to_right[:], frac)
+                step = PAIR if (b, g) == (BLOCKS - 1, PASSES - 1) else PACK
+                for j in range(0, PACK, step):
+                    nc.sync.dma_start(w_raw[b, g][:, j : j + step, :], w_rows[g, :, j : j + step, b * P : (b + 1) * P])
         left_sb = keep([P, V // PER_COLUMN], U16, name="left_sb")
         nc.sync.dma_start(left_sb[:], left)
         right_sb = keep([P, V // PER_COLUMN], U16, name="right_sb")
         nc.sync.dma_start(right_sb[:], right)
+        to_right = keep([P, V], F32, name="to_right")
+        nc.sync.dma_start(to_right[:], frac)
 
         def quantize(codes, scales, grouped):
             nc.vector.quantize_mx(out=codes.bitcast(FP8X4), scales=scales, in_=grouped.rearrange("p n j -> p (n j)"))
@@ -74,11 +77,26 @@ def tile_picked_lerp_none_e_kernel(tc, xT, w1, frac, offs, left, right, out):
         quarters = [slice(q * QUARTER, (q + 1) * QUARTER) for q in range(4)]
         x_codes, x_scales = {}, {}
 
-        grouped0 = keep([P, S, PACK], BF16, name="grouped0")
-        picked0 = keep([P, PACK, S], F32, name="picked0")
-        for j in range(PACK):
-            nc.vector.tensor_copy(picked0[:, j, :], planes[0, j].indirect(offs_sb[:]))
-        weave(nc.scalar.copy, grouped0[:], picked0[:])
+        def entries(cols):
+            return offs_sb[:, cols.start // PER_COLUMN : cols.stop // PER_COLUMN]
+
+        grouped0 = [keep([P, HALF, PACK], BF16, name=f"grouped0{h}") for h in range(2)]
+        first_pair = keep([P, PAIR, S], F32, name="first_pair")
+        for j in range(PAIR):
+            nc.vector.tensor_copy(first_pair[:, j, :], planes[0, j].indirect(offs_sb[:]))
+        for h, cols in enumerate(halves):
+            weave(nc.scalar.copy, grouped0[h][:, :, 0:PAIR], first_pair[:, :, cols])
+        codes0 = keep([P, S], U32, name="codes0")
+        scales0 = keep([P, S], U8, name="scales0")
+        second_pair = [keep([P, PAIR, HALF], F32, name=f"second_pair{h}") for h in range(2)]
+        for h, cols in enumerate(halves):
+            for j in range(PAIR):
+                nc.vector.tensor_copy(second_pair[h][:, j, :], planes[0, PAIR + j].indirect(entries(cols)))
+            weave(nc.scalar.copy, grouped0[h][:, :, PAIR:PACK], second_pair[h][:])
+        for h, cols in enumerate(halves):
+            quantize(codes0[:, cols], scales0[:, cols], grouped0[h][:])
+        for q, cols in enumerate(quarters):
+            x_codes[0, q], x_scales[0, q] = codes0[:, cols], scales0[:, cols]
 
         grouped1 = [keep([P, HALF, PACK], BF16, name=f"grouped1{h}") for h in range(2)]
         picked1 = keep([P, PAIR, S], F32, name="picked1")
@@ -86,15 +104,9 @@ def tile_picked_lerp_none_e_kernel(tc, xT, w1, frac, offs, left, right, out):
             nc.vector.tensor_copy(picked1[:, j, :], planes[1, j].indirect(offs_sb[:]))
         for h, cols in enumerate(halves):
             weave(nc.scalar.copy, grouped1[h][:, :, 0:PAIR], picked1[:, :, cols])
-        codes0 = keep([P, S], U32, name="codes0", tag="planes11")
-        scales0 = keep([P, S], U8, name="scales0")
-        quantize(codes0[:], scales0[:], grouped0[:])
-        for q, cols in enumerate(quarters):
-            x_codes[0, q], x_scales[0, q] = codes0[:, cols], scales0[:, cols]
         for j in range(PAIR, PACK):
             for h, cols in enumerate(halves):
-                entries = offs_sb[:, cols.start // PER_COLUMN : cols.stop // PER_COLUMN]
-                nc.vector.tensor_copy(grouped1[h][:, :, j], planes[1, j].indirect(entries))
+                nc.vector.tensor_copy(grouped1[h][:, :, j], planes[1, j].indirect(entries(cols)))
 
         w_grouped, w_codes, w_scales = {}, {}, {}
 
@@ -165,9 +177,9 @@ def tile_picked_lerp_none_e_kernel(tc, xT, w1, frac, offs, left, right, out):
         for b in range(BLOCKS):
             from_left.append(keep([P, V], F32, name=f"from_left{b}"))
             from_right.append(keep([P, V], F32, name=f"from_right{b}"))
-            nc.vector.tensor_tensor(from_left[b][:], y[b][:].indirect(left_sb[:]), to_left[:], MULT)
             nc.vector.tensor_tensor(from_right[b][:], y[b][:].indirect(right_sb[:]), to_right[:], MULT)
-        mixed = [keep([P, V], F32, name="mixed0", tag="w_grouped10"), keep([P, V], F32, name="mixed1")]
+            nc.vector.tensor_tensor(from_left[b][:], y[b][:].indirect(left_sb[:]), to_left[:], MULT)
+        mixed = [keep([P, V], F32, name="mixed0", tag="to_right"), keep([P, V], F32, name="mixed1")]
         for b in range(BLOCKS):
             nc.vector.tensor_tensor(mixed[b][:], from_left[b][:], from_right[b][:], ADD)
             nc.sync.dma_start(out[b * P : (b + 1) * P, :], mixed[b][:])

@@ -13,6 +13,7 @@ U8 = mybir.dt.uint8
 FP8X4 = mybir.dt.float8_e4m3fn_x4
 MULT = mybir.AluOpType.mult
 ADD = mybir.AluOpType.add
+COPY = mybir.ActivationFunctionType.Copy
 
 P = 128
 PACK = 4
@@ -55,7 +56,9 @@ def tile_picked_lerp_none_e_kernel(tc, xT, w1, frac, offs, left, right, out):
         load_planes(0, PAIR, PAIR)
         load_planes(1, 0, PAIR)
         for j in range(PAIR, PACK):
-            load_planes(1, j, 1)
+            tile = keep([P, T], F32, name=f"plane1{j}")
+            nc.sync.dma_start(tile[:], x_rows[1, :, j, :])
+            planes[1, j] = tile[:]
         w_raw = {}
         for b in range(BLOCKS):
             for g in range(PASSES):
@@ -98,15 +101,19 @@ def tile_picked_lerp_none_e_kernel(tc, xT, w1, frac, offs, left, right, out):
         for q, cols in enumerate(quarters):
             x_codes[0, q], x_scales[0, q] = codes0[:, cols], scales0[:, cols]
 
-        grouped1 = [keep([P, HALF, PACK], BF16, name=f"grouped1{h}") for h in range(2)]
+        near, far = slice(0, S - QUARTER), quarters[3]
+        grouped_near = keep([P, S - QUARTER, PACK], BF16, name="grouped_near")
+        grouped_far = keep([P, QUARTER, PACK], BF16, name="grouped_far")
         picked1 = keep([P, PAIR, S], F32, name="picked1")
         for j in range(PAIR):
             nc.vector.tensor_copy(picked1[:, j, :], planes[1, j].indirect(offs_sb[:]))
-        for h, cols in enumerate(halves):
-            weave(nc.scalar.copy, grouped1[h][:, :, 0:PAIR], picked1[:, :, cols])
+        weave(nc.scalar.copy, grouped_near[:, :, 0:PAIR], picked1[:, :, near])
+        weave(nc.scalar.copy, grouped_far[:, :, 0:PAIR], picked1[:, :, far])
+        far_pair = keep([P, PAIR, QUARTER], F32, name="far_pair")
         for j in range(PAIR, PACK):
-            for h, cols in enumerate(halves):
-                nc.vector.tensor_copy(grouped1[h][:, :, j], planes[1, j].indirect(entries(cols)))
+            nc.vector.tensor_copy(grouped_near[:, :, j], planes[1, j].indirect(entries(near)))
+            nc.scalar.activation(far_pair[:, j - PAIR, :], planes[1, j].indirect(entries(far)), COPY)
+        weave(nc.vector.tensor_copy, grouped_far[:, :, PAIR:PACK], far_pair[:])
 
         w_grouped, w_codes, w_scales = {}, {}, {}
 
@@ -124,7 +131,8 @@ def tile_picked_lerp_none_e_kernel(tc, xT, w1, frac, offs, left, right, out):
             scales = keep([P, HALF], U8, name=f"scales1{h}")
             for i in range(2):
                 cols = slice(i * QUARTER, (i + 1) * QUARTER)
-                quantize(codes[:, cols], scales[:, cols], grouped1[h][:, cols, :])
+                q = 2 * h + i
+                quantize(codes[:, cols], scales[:, cols], grouped_far[:] if q == 3 else grouped_near[:, quarters[q], :])
                 x_codes[1, 2 * h + i], x_scales[1, 2 * h + i] = codes[:, cols], scales[:, cols]
 
         acc = {(b, q): psum.tile([P, QUARTER], F32, name=f"acc{b}{q}") for b in range(BLOCKS) for q in range(4)}

@@ -181,12 +181,20 @@ def tile_picked_lerp_none_e_kernel(tc, xT, w1, frac, offs, left, right, out):
             for q, cols in enumerate(quarters):
                 nc.scalar.copy(y[b][:, cols], acc[b, q][:])
 
-        from_left, from_right = [], []
-        for b in range(BLOCKS):
-            from_left.append(keep([P, V], F32, name=f"from_left{b}"))
-            from_right.append(keep([P, V], F32, name=f"from_right{b}"))
-            nc.vector.tensor_tensor(from_right[b][:], y[b][:].indirect(right_sb[:]), to_right[:], MULT)
-            nc.vector.tensor_tensor(from_left[b][:], y[b][:].indirect(left_sb[:]), to_left[:], MULT)
+        first, second = slice(0, V // 2), slice(V // 2, V)
+        from_left = [keep([P, V], F32, name=f"from_left{b}") for b in range(BLOCKS)]
+        from_right = [keep([P, V], F32, name=f"from_right{b}") for b in range(BLOCKS)]
+        at_left = keep([P, V // 2], F32, name="at_left")
+
+        def left_entries(cols):
+            return left_sb[:, cols.start // PER_COLUMN : cols.stop // PER_COLUMN]
+
+        nc.vector.tensor_tensor(from_right[0][:], y[0][:].indirect(right_sb[:]), to_right[:], MULT)
+        nc.vector.tensor_tensor(from_left[0][:], y[0][:].indirect(left_sb[:]), to_left[:], MULT)
+        nc.scalar.activation(at_left[:], y[1][:].indirect(left_entries(first)), COPY)
+        nc.vector.tensor_tensor(from_right[1][:], y[1][:].indirect(right_sb[:]), to_right[:], MULT)
+        nc.vector.tensor_tensor(from_left[1][:, second], y[1][:].indirect(left_entries(second)), to_left[:, second], MULT)
+        nc.vector.tensor_tensor(from_left[1][:, first], at_left[:], to_left[:, first], MULT)
         mixed = [keep([P, V], F32, name="mixed0", tag="to_right"), keep([P, V], F32, name="mixed1")]
         for b in range(BLOCKS):
             nc.vector.tensor_tensor(mixed[b][:], from_left[b][:], from_right[b][:], ADD)

@@ -63,15 +63,14 @@ def tile_picked_lerp_none_e_kernel(tc, xT, w1, frac, offs, left, right, out):
         for b in range(BLOCKS):
             for g in range(PASSES):
                 w_raw[b, g] = keep([P, PACK, P], F32, name=f"w_raw{b}{g}")
-                step = PAIR if (b, g) == (BLOCKS - 1, PASSES - 1) else PACK
-                for j in range(0, PACK, step):
-                    nc.sync.dma_start(w_raw[b, g][:, j : j + step, :], w_rows[g, :, j : j + step, b * P : (b + 1) * P])
+                nc.sync.dma_start(w_raw[b, g][:], w_rows[g, :, :, b * P : (b + 1) * P])
         left_sb = keep([P, V // PER_COLUMN], U16, name="left_sb")
         nc.sync.dma_start(left_sb[:], left)
         right_sb = keep([P, V // PER_COLUMN], U16, name="right_sb")
         nc.sync.dma_start(right_sb[:], right)
         to_right = keep([P, V], F32, name="to_right")
-        nc.sync.dma_start(to_right[:], frac)
+        for cols in (slice(0, V // 2), slice(V // 2, V)):
+            nc.sync.dma_start(to_right[:, cols], frac[:, cols])
 
         def quantize(codes, scales, grouped):
             nc.vector.quantize_mx(out=codes.bitcast(FP8X4), scales=scales, in_=grouped.rearrange("p n j -> p (n j)"))
@@ -167,12 +166,12 @@ def tile_picked_lerp_none_e_kernel(tc, xT, w1, frac, offs, left, right, out):
         column_halves = [slice(0, P // 2), slice(P // 2, P)]
         for cols in column_halves:
             weave(nc.vector.tensor_copy, w_grouped[1, 1][:, cols, :], w_raw[1, 1][:, :, cols])
-        to_left = keep([P, V], F32, name="to_left", tag="w_grouped10")
-        nc.vector.tensor_scalar(to_left[:], to_right[:], -1.0, 1.0, MULT, ADD)
         w_codes[1, 1] = keep([P, P], U32, name="w_codes11")
         w_scales[1, 1] = keep([P, P], U8, name="w_scales11")
         for cols in column_halves:
             quantize(w_codes[1, 1][:, cols], w_scales[1, 1][:, cols], w_grouped[1, 1][:, cols, :])
+        to_left = keep([P, V], F32, name="to_left")
+        nc.vector.tensor_scalar(to_left[:], to_right[:], -1.0, 1.0, MULT, ADD)
         multiply(1, 1, 0)
         multiply(1, 1, 1)
 

@@ -103,11 +103,13 @@ def tile_picked_lerp_none_e_kernel(tc, xT, w1, frac, offs, left, right, out):
         near, far = slice(0, S - QUARTER), quarters[3]
         grouped_near = keep([P, S - QUARTER, PACK], BF16, name="grouped_near")
         grouped_far = keep([P, QUARTER, PACK], BF16, name="grouped_far")
-        picked1 = keep([P, PAIR, S], F32, name="picked1")
-        for j in range(PAIR):
-            nc.vector.tensor_copy(picked1[:, j, :], planes[1, j].indirect(offs_sb[:]))
-        weave(nc.scalar.copy, grouped_near[:, :, 0:PAIR], picked1[:, :, near])
-        weave(nc.scalar.copy, grouped_far[:, :, 0:PAIR], picked1[:, :, far])
+        picked1 = [keep([P, PAIR, HALF], F32, name=f"picked1{h}") for h in range(2)]
+        for h, cols in enumerate(halves):
+            for j in range(PAIR):
+                nc.vector.tensor_copy(picked1[h][:, j, :], planes[1, j].indirect(entries(cols)))
+        weave(nc.scalar.copy, grouped_near[:, halves[0], 0:PAIR], picked1[0][:])
+        weave(nc.scalar.copy, grouped_near[:, quarters[2], 0:PAIR], picked1[1][:, :, quarters[0]])
+        weave(nc.scalar.copy, grouped_far[:, :, 0:PAIR], picked1[1][:, :, quarters[1]])
         far_pair = keep([P, PAIR, QUARTER], F32, name="far_pair")
         for j in range(PAIR, PACK):
             nc.vector.tensor_copy(grouped_near[:, :, j], planes[1, j].indirect(entries(near)))

@@ -23,6 +23,7 @@ BLOCKS = N // P
 HALF = S // 2
 QUARTER = S // 4
 PER_COLUMN = 16
+ON_SCALAR = 192
 LINE = 2
 ALIGN = 256
 
@@ -182,10 +183,10 @@ def tile_picked_lerp_none_e_kernel(tc, xT, w1, frac, offs, left, right, out):
             for q, cols in enumerate(quarters):
                 nc.scalar.copy(y[b][:, cols], acc[b, q][:])
 
-        first, second = slice(0, V // 2), slice(V // 2, V)
+        first, second = slice(0, ON_SCALAR), slice(ON_SCALAR, V)
         from_left = [keep([P, V], F32, name=f"from_left{b}") for b in range(BLOCKS)]
         from_right = [keep([P, V], F32, name=f"from_right{b}") for b in range(BLOCKS)]
-        at_left = keep([P, V // 2], F32, name="at_left")
+        at_left = keep([P, ON_SCALAR], F32, name="at_left")
 
         def left_entries(cols):
             return left_sb[:, cols.start // PER_COLUMN : cols.stop // PER_COLUMN]

@@ -24,6 +24,7 @@ HALF = S // 2
 QUARTER = S // 4
 PER_COLUMN = 16
 ON_SCALAR = 192
+FAR = 192
 LINE = 2
 ALIGN = 256
 
@@ -101,21 +102,19 @@ def tile_picked_lerp_none_e_kernel(tc, xT, w1, frac, offs, left, right, out):
         for q, cols in enumerate(quarters):
             x_codes[0, q], x_scales[0, q] = codes0[:, cols], scales0[:, cols]
 
-        near, far = slice(0, S - QUARTER), quarters[3]
-        grouped_near = keep([P, S - QUARTER, PACK], BF16, name="grouped_near")
-        grouped_far = keep([P, QUARTER, PACK], BF16, name="grouped_far")
+        near, far = slice(0, S - FAR), slice(S - FAR, S)
+        grouped1 = keep([P, S, PACK], BF16, name="grouped1")
         picked1 = [keep([P, PAIR, HALF], F32, name=f"picked1{h}") for h in range(2)]
         for h, cols in enumerate(halves):
             for j in range(PAIR):
                 nc.vector.tensor_copy(picked1[h][:, j, :], planes[1, j].indirect(entries(cols)))
-        weave(nc.scalar.copy, grouped_near[:, halves[0], 0:PAIR], picked1[0][:])
-        weave(nc.scalar.copy, grouped_near[:, quarters[2], 0:PAIR], picked1[1][:, :, quarters[0]])
-        weave(nc.scalar.copy, grouped_far[:, :, 0:PAIR], picked1[1][:, :, quarters[1]])
-        far_pair = keep([P, PAIR, QUARTER], F32, name="far_pair")
+        for h, cols in enumerate(halves):
+            weave(nc.scalar.copy, grouped1[:, cols, 0:PAIR], picked1[h][:])
+        far_pair = keep([P, PAIR, FAR], F32, name="far_pair")
         for j in range(PAIR, PACK):
-            nc.vector.tensor_copy(grouped_near[:, :, j], planes[1, j].indirect(entries(near)))
+            nc.vector.tensor_copy(grouped1[:, near, j], planes[1, j].indirect(entries(near)))
             nc.scalar.activation(far_pair[:, j - PAIR, :], planes[1, j].indirect(entries(far)), COPY)
-        weave(nc.vector.tensor_copy, grouped_far[:, :, PAIR:PACK], far_pair[:])
+        weave(nc.vector.tensor_copy, grouped1[:, far, PAIR:PACK], far_pair[:])
 
         w_grouped, w_codes, w_scales = {}, {}, {}
 
@@ -134,7 +133,7 @@ def tile_picked_lerp_none_e_kernel(tc, xT, w1, frac, offs, left, right, out):
             for i in range(2):
                 cols = slice(i * QUARTER, (i + 1) * QUARTER)
                 q = 2 * h + i
-                quantize(codes[:, cols], scales[:, cols], grouped_far[:] if q == 3 else grouped_near[:, quarters[q], :])
+                quantize(codes[:, cols], scales[:, cols], grouped1[:, quarters[q], :])
                 x_codes[1, 2 * h + i], x_scales[1, 2 * h + i] = codes[:, cols], scales[:, cols]
 
         acc = {(b, q): psum.tile([P, QUARTER], F32, name=f"acc{b}{q}") for b in range(BLOCKS) for q in range(4)}

@@ -24,7 +24,7 @@ HALF = S // 2
 QUARTER = S // 4
 PER_COLUMN = 16
 ON_SCALAR = 192
-FAR = 192
+FAR = 224
 LINE = 2
 ALIGN = 256
 
@@ -105,9 +105,10 @@ def tile_picked_lerp_none_e_kernel(tc, xT, w1, frac, offs, left, right, out):
         near, far = slice(0, S - FAR), slice(S - FAR, S)
         grouped1 = keep([P, S, PACK], BF16, name="grouped1")
         picked1 = [keep([P, PAIR, HALF], F32, name=f"picked1{h}") for h in range(2)]
-        for h, cols in enumerate(halves):
-            for j in range(PAIR):
-                nc.vector.tensor_copy(picked1[h][:, j, :], planes[1, j].indirect(entries(cols)))
+        nc.scalar.activation(picked1[0][:, 1, :], planes[1, 1].indirect(entries(halves[0])), COPY)
+        nc.vector.tensor_copy(picked1[0][:, 0, :], planes[1, 0].indirect(entries(halves[0])))
+        for j in range(PAIR):
+            nc.vector.tensor_copy(picked1[1][:, j, :], planes[1, j].indirect(entries(halves[1])))
         for h, cols in enumerate(halves):
             weave(nc.scalar.copy, grouped1[:, cols, 0:PAIR], picked1[h][:])
         far_pair = keep([P, PAIR, FAR], F32, name="far_pair")

@@ -24,7 +24,7 @@ HALF = S // 2
 QUARTER = S // 4
 PER_COLUMN = 16
 ON_SCALAR = 192
-FAR = 224
+FAR = 256
 LINE = 2
 ALIGN = 256
 
@@ -111,11 +111,9 @@ def tile_picked_lerp_none_e_kernel(tc, xT, w1, frac, offs, left, right, out):
             nc.vector.tensor_copy(picked1[1][:, j, :], planes[1, j].indirect(entries(halves[1])))
         for h, cols in enumerate(halves):
             weave(nc.scalar.copy, grouped1[:, cols, 0:PAIR], picked1[h][:])
-        far_pair = keep([P, PAIR, FAR], F32, name="far_pair")
         for j in range(PAIR, PACK):
             nc.vector.tensor_copy(grouped1[:, near, j], planes[1, j].indirect(entries(near)))
-            nc.scalar.activation(far_pair[:, j - PAIR, :], planes[1, j].indirect(entries(far)), COPY)
-        weave(nc.vector.tensor_copy, grouped1[:, far, PAIR:PACK], far_pair[:])
+            nc.scalar.activation(grouped1[:, far, j], planes[1, j].indirect(entries(far)), COPY)
 
         w_grouped, w_codes, w_scales = {}, {}, {}
 

@@ -24,7 +24,7 @@ HALF = S // 2
 QUARTER = S // 4
 PER_COLUMN = 16
 ON_SCALAR = 192
-FAR = 256
+FAR = 160
 LINE = 2
 ALIGN = 256
 

@@ -116,15 +116,18 @@ def tile_picked_lerp_none_e_kernel(tc, xT, w1, frac, offs, left, right, out):
             nc.scalar.activation(grouped1[:, far, j], planes[1, j].indirect(entries(far)), COPY)
 
         w_grouped, w_codes, w_scales = {}, {}, {}
+        column_halves = [slice(0, P // 2), slice(P // 2, P)]
 
         def group_w(b, g, copy, tag=""):
             w_grouped[b, g] = keep([P, P, PACK], BF16, name=f"w_grouped{b}{g}", tag=tag)
-            weave(copy, w_grouped[b, g][:], w_raw[b, g][:])
+            for cols in column_halves:
+                weave(copy, w_grouped[b, g][:, cols, :], w_raw[b, g][:, :, cols])
 
         def quantize_w(b, g):
             w_codes[b, g] = keep([P, P], U32, name=f"w_codes{b}{g}")
             w_scales[b, g] = keep([P, P], U8, name=f"w_scales{b}{g}")
-            quantize(w_codes[b, g][:], w_scales[b, g][:], w_grouped[b, g][:])
+            for cols in column_halves:
+                quantize(w_codes[b, g][:, cols], w_scales[b, g][:, cols], w_grouped[b, g][:, cols, :])
 
         def quantize_half(h):
             codes = keep([P, HALF], U32, name=f"codes1{h}", tag=f"w_raw0{h}")
@@ -164,7 +167,6 @@ def tile_picked_lerp_none_e_kernel(tc, xT, w1, frac, offs, left, right, out):
         multiply(1, 0, 0)
         multiply(1, 0, 1)
         w_grouped[1, 1] = keep([P, P, PACK], BF16, name="w_grouped11", tag="w_raw10")
-        column_halves = [slice(0, P // 2), slice(P // 2, P)]
         for cols in column_halves:
             weave(nc.vector.tensor_copy, w_grouped[1, 1][:, cols, :], w_raw[1, 1][:, :, cols])
         w_codes[1, 1] = keep([P, P], U32, name="w_codes11")

from contextlib import ExitStack

import concourse.mybir as mybir

K, T, S, V, N = 1024, 2048, 512, 256, 256
FLOPS = 2 * K * S * N

F32 = mybir.dt.float32
BF16 = mybir.dt.bfloat16
U32 = mybir.dt.uint32
U16 = mybir.dt.uint16
U8 = mybir.dt.uint8
FP8X4 = mybir.dt.float8_e4m3fn_x4
MULT = mybir.AluOpType.mult
ADD = mybir.AluOpType.add
COPY = mybir.ActivationFunctionType.Copy

P = 128
PACK = 4
PAIR = 2
PASSES = K // (P * PACK)
BLOCKS = N // P
HALF = S // 2
QUARTER = S // 4
PER_COLUMN = 16
ON_SCALAR = 192
FAR = 160
LINE = 2
ALIGN = 256


def weave(copy, grouped, rows):
    copy(grouped.rearrange("p (c i) j -> p c j i", i=LINE), rows.rearrange("p j (c i) -> p c j i", i=LINE))


def tile_picked_lerp_none_e_kernel(tc, xT, w1, frac, offs, left, right, out):
    nc = tc.nc
    with ExitStack() as ctx:
        pool = ctx.enter_context(tc.tile_pool(name="keep", bufs=1))
        psum = ctx.enter_context(tc.psum_pool(name="psum", bufs=1))

        def keep(shape, dtype, name, tag=""):
            return pool.tile(shape, dtype, name=name, tag=tag, align_bytes=ALIGN)

        x_rows = xT.rearrange("(g p j) t -> g p j t", p=P, j=PACK)
        w_rows = w1.rearrange("(g p j) m -> g p j m", p=P, j=PACK)
        planes = {}

        def load_planes(g, j0, count):
            tile = keep([P, count, T], F32, name=f"planes{g}{j0}")
            nc.sync.dma_start(tile[:], x_rows[g, :, j0 : j0 + count, :])
            for j in range(count):
                planes[g, j0 + j] = tile[:, j, :]

        load_planes(0, 0, PAIR)
        offs_sb = keep([P, S // PER_COLUMN], U16, name="offs_sb")
        nc.sync.dma_start(offs_sb[:], offs)
        load_planes(0, PAIR, PAIR)
        load_planes(1, 0, PAIR)
        for j in range(PAIR, PACK):
            tile = keep([P, T], F32, name=f"plane1{j}")
            nc.sync.dma_start(tile[:], x_rows[1, :, j, :])
            planes[1, j] = tile[:]
        w_raw = {}
        for b in range(BLOCKS):
            for g in range(PASSES):
                w_raw[b, g] = keep([P, PACK, P], F32, name=f"w_raw{b}{g}")
                nc.sync.dma_start(w_raw[b, g][:], w_rows[g, :, :, b * P : (b + 1) * P])
        left_sb = keep([P, V // PER_COLUMN], U16, name="left_sb")
        nc.sync.dma_start(left_sb[:], left)
        right_sb = keep([P, V // PER_COLUMN], U16, name="right_sb")
        nc.sync.dma_start(right_sb[:], right)
        to_right = keep([P, V], F32, name="to_right")
        for cols in (slice(0, V // 2), slice(V // 2, V)):
            nc.sync.dma_start(to_right[:, cols], frac[:, cols])

        def quantize(codes, scales, grouped):
            nc.vector.quantize_mx(out=codes.bitcast(FP8X4), scales=scales, in_=grouped.rearrange("p n j -> p (n j)"))

        halves = [slice(0, HALF), slice(HALF, S)]
        quarters = [slice(q * QUARTER, (q + 1) * QUARTER) for q in range(4)]
        x_codes, x_scales = {}, {}

        def entries(cols):
            return offs_sb[:, cols.start // PER_COLUMN : cols.stop // PER_COLUMN]

        grouped0 = [keep([P, HALF, PACK], BF16, name=f"grouped0{h}") for h in range(2)]
        first_pair = keep([P, PAIR, S], F32, name="first_pair")
        for j in range(PAIR):
            nc.vector.tensor_copy(first_pair[:, j, :], planes[0, j].indirect(offs_sb[:]))
        for h, cols in enumerate(halves):
            weave(nc.scalar.copy, grouped0[h][:, :, 0:PAIR], first_pair[:, :, cols])
        codes0 = keep([P, S], U32, name="codes0")
        scales0 = keep([P, S], U8, name="scales0")
        second_pair = [keep([P, PAIR, HALF], F32, name=f"second_pair{h}") for h in range(2)]
        for h, cols in enumerate(halves):
            for j in range(PAIR):
                nc.vector.tensor_copy(second_pair[h][:, j, :], planes[0, PAIR + j].indirect(entries(cols)))
            weave(nc.scalar.copy, grouped0[h][:, :, PAIR:PACK], second_pair[h][:])
        for h, cols in enumerate(halves):
            quantize(codes0[:, cols], scales0[:, cols], grouped0[h][:])
        for q, cols in enumerate(quarters):
            x_codes[0, q], x_scales[0, q] = codes0[:, cols], scales0[:, cols]

        near, far = slice(0, S - FAR), slice(S - FAR, S)
        grouped1 = keep([P, S, PACK], BF16, name="grouped1")
        picked1 = [keep([P, PAIR, HALF], F32, name=f"picked1{h}") for h in range(2)]
        nc.scalar.activation(picked1[0][:, 1, :], planes[1, 1].indirect(entries(halves[0])), COPY)
        nc.vector.tensor_copy(picked1[0][:, 0, :], planes[1, 0].indirect(entries(halves[0])))
        for j in range(PAIR):
            nc.vector.tensor_copy(picked1[1][:, j, :], planes[1, j].indirect(entries(halves[1])))
        for h, cols in enumerate(halves):
            weave(nc.scalar.copy, grouped1[:, cols, 0:PAIR], picked1[h][:])
        for j in range(PAIR, PACK):
            nc.vector.tensor_copy(grouped1[:, near, j], planes[1, j].indirect(entries(near)))
            nc.scalar.activation(grouped1[:, far, j], planes[1, j].indirect(entries(far)), COPY)

        w_grouped, w_codes, w_scales = {}, {}, {}
        column_halves = [slice(0, P // 2), slice(P // 2, P)]

        def group_w(b, g, copy, tag=""):
            w_grouped[b, g] = keep([P, P, PACK], BF16, name=f"w_grouped{b}{g}", tag=tag)
            for cols in column_halves:
                weave(copy, w_grouped[b, g][:, cols, :], w_raw[b, g][:, :, cols])

        def quantize_w(b, g):
            w_codes[b, g] = keep([P, P], U32, name=f"w_codes{b}{g}")
            w_scales[b, g] = keep([P, P], U8, name=f"w_scales{b}{g}")
            for cols in column_halves:
                quantize(w_codes[b, g][:, cols], w_scales[b, g][:, cols], w_grouped[b, g][:, cols, :])

        def quantize_half(h):
            codes = keep([P, HALF], U32, name=f"codes1{h}", tag=f"w_raw0{h}")
            scales = keep([P, HALF], U8, name=f"scales1{h}")
            for i in range(2):
                cols = slice(i * QUARTER, (i + 1) * QUARTER)
                q = 2 * h + i
                quantize(codes[:, cols], scales[:, cols], grouped1[:, quarters[q], :])
                x_codes[1, 2 * h + i], x_scales[1, 2 * h + i] = codes[:, cols], scales[:, cols]

        acc = {(b, q): psum.tile([P, QUARTER], F32, name=f"acc{b}{q}") for b in range(BLOCKS) for q in range(4)}

        def multiply(b, g, h):
            for q in (2 * h, 2 * h + 1):
                nc.tensor.matmul_mx(
                    out=acc[b, q][:],
                    lhsT=w_codes[b, g][:].bitcast(FP8X4),
                    lhsT_scale=w_scales[b, g][:],
                    rhs=x_codes[g, q].bitcast(FP8X4),
                    rhs_scale=x_scales[g, q],
                    start=(g == 0),
                    stop=(g == PASSES - 1),
                )

        group_w(0, 0, nc.scalar.copy)
        group_w(0, 1, nc.scalar.copy)
        group_w(1, 0, nc.scalar.copy)
        quantize_w(0, 0)
        multiply(0, 0, 0)
        multiply(0, 0, 1)
        quantize_half(0)
        quantize_w(0, 1)
        multiply(0, 1, 0)
        quantize_half(1)
        multiply(0, 1, 1)
        quantize_w(1, 0)
        multiply(1, 0, 0)
        multiply(1, 0, 1)
        w_grouped[1, 1] = keep([P, P, PACK], BF16, name="w_grouped11", tag="w_raw10")
        for cols in column_halves:
            weave(nc.vector.tensor_copy, w_grouped[1, 1][:, cols, :], w_raw[1, 1][:, :, cols])
        w_codes[1, 1] = keep([P, P], U32, name="w_codes11")
        w_scales[1, 1] = keep([P, P], U8, name="w_scales11")
        for cols in column_halves:
            quantize(w_codes[1, 1][:, cols], w_scales[1, 1][:, cols], w_grouped[1, 1][:, cols, :])
        to_left = keep([P, V], F32, name="to_left")
        nc.vector.tensor_scalar(to_left[:], to_right[:], -1.0, 1.0, MULT, ADD)
        multiply(1, 1, 0)
        multiply(1, 1, 1)

        y = [keep([P, S], F32, name=f"y{b}") for b in range(BLOCKS)]
        for b in range(BLOCKS):
            for q, cols in enumerate(quarters):
                nc.scalar.copy(y[b][:, cols], acc[b, q][:])

        first, second = slice(0, ON_SCALAR), slice(ON_SCALAR, V)
        from_left = [keep([P, V], F32, name=f"from_left{b}") for b in range(BLOCKS)]
        from_right = [keep([P, V], F32, name=f"from_right{b}") for b in range(BLOCKS)]
        at_left = keep([P, ON_SCALAR], F32, name="at_left")

        def left_entries(cols):
            return left_sb[:, cols.start // PER_COLUMN : cols.stop // PER_COLUMN]

        nc.vector.tensor_tensor(from_right[0][:], y[0][:].indirect(right_sb[:]), to_right[:], MULT)
        nc.vector.tensor_tensor(from_left[0][:], y[0][:].indirect(left_sb[:]), to_left[:], MULT)
        nc.scalar.activation(at_left[:], y[1][:].indirect(left_entries(first)), COPY)
        nc.vector.tensor_tensor(from_right[1][:], y[1][:].indirect(right_sb[:]), to_right[:], MULT)
        nc.vector.tensor_tensor(from_left[1][:, second], y[1][:].indirect(left_entries(second)), to_left[:, second], MULT)
        nc.vector.tensor_tensor(from_left[1][:, first], at_left[:], to_left[:, first], MULT)
        mixed = [keep([P, V], F32, name="mixed0", tag="to_right"), keep([P, V], F32, name="mixed1")]
        for b in range(BLOCKS):
            nc.vector.tensor_tensor(mixed[b][:], from_left[b][:], from_right[b][:], ADD)
            nc.sync.dma_start(out[b * P : (b + 1) * P, :], mixed[b][:])
